import numpy as np
import ml_dtypes


def mxq(x, axis, fmt="e4m3"):
    dtype, down = {"e4m3": (ml_dtypes.float8_e4m3fn, 7), "e5m2": (ml_dtypes.float8_e5m2, 14)}[fmt]
    v = np.moveaxis(np.asarray(x, np.float32).astype(ml_dtypes.bfloat16).astype(np.float64), axis, -1)
    blocks = v.reshape(v.shape[:-1] + (-1, 32))
    amax = np.abs(blocks).max(-1, keepdims=True)
    byte = np.maximum(np.where(amax > 0, np.frexp(amax)[1] - 1 + 127, 0) - down, 1)
    scale = np.exp2(byte - 127.0)
    codes = (blocks / scale).astype(np.float32).astype(dtype).astype(np.float64)
    return np.moveaxis((codes * scale).reshape(v.shape), -1, axis)


WIDE = False


def mx_kscale(k):
    if not WIDE:
        return np.ones(k)
    levels = np.array([10, -10, 5, -5, 0])
    if k % 512:
        return np.exp2(np.random.permutation(np.resize(levels, k // 32))).repeat(32)
    a = np.empty((k // 512, 16))
    for p in range(k // 512):
        a[p, :8] = np.random.permutation(np.resize(levels, 8))
        for g in range(8):
            far = levels[np.abs(levels - a[p, g]) >= 10]
            a[p, g + 8] = far[np.random.randint(len(far))]
    return np.exp2(a.ravel()).repeat(32)


def f64(x):
    return np.asarray(x).astype(np.float64)


def striped(idx):
    return np.tile(idx.reshape(-1, 16).T, (8, 1)).astype(np.uint16)


def unstriped(offs):
    return offs[:16].T.reshape(-1).astype(np.int64)


def pack_weight(w):
    k, n = w.shape
    w = f64(np.asarray(w, np.float32).astype(ml_dtypes.bfloat16)).reshape(k // 32, 32, n)
    amax = np.abs(w).max(1)
    byte = np.clip(np.where(amax > 0, np.frexp(amax)[1] - 1 + 127 - 7, 1), 1, 254)
    scaled = (w * np.exp2(127.0 - byte)[:, None, :]).reshape(k, n).astype(np.float32)
    words = np.ascontiguousarray(scaled.reshape(k // 512, 128, 4, n).transpose(0, 1, 3, 2)).astype(ml_dtypes.float8_e4m3fn).view(np.uint8)
    return words, np.ascontiguousarray(byte.astype(np.uint8).reshape(k // 512, 16, n))


def unpack_weight(words, scales):
    g, p, n, _ = words.shape
    vals = np.ascontiguousarray(words).view(ml_dtypes.float8_e4m3fn).astype(np.float64) * np.repeat(np.exp2(scales.astype(np.float64) - 127.0), 8, axis=1)[..., None]
    return vals.transpose(0, 1, 3, 2).reshape(g * 512, n)


K, T, S, H, N = 512, 4096, 1024, 512, 128


def setup_inputs():
    n = np.random.standard_normal
    s = mx_kscale(K)[:, None]
    u = mx_kscale(H)
    packed_xT = pack_weight(n((K, T)) * s)
    packed_w2 = pack_weight(n((H, N)) / np.sqrt(H) / u[:, None])
    return {
        "x_words": packed_xT[0],
        "x_scales": packed_xT[1],
        "w1": (n((K, H)) / np.sqrt(K) / s).astype(np.float32),
        "w2_words": packed_w2[0],
        "w2_scales": packed_w2[1],
        "gamma": (np.random.uniform(0.5, 1.5, (H, 1)) * u[:, None]).astype(np.float32),
        "offs": striped(np.random.permutation(T)[:S]),
    }


def reference(x_words, x_scales, w1, w2_words, w2_scales, gamma, offs):
    xq = unpack_weight(x_words, x_scales)[:, unstriped(offs)]
    h = mxq(f64(w1), 0, "e4m3").T @ xq
    hn = (h - h.mean(axis=1, keepdims=True)) / np.sqrt(h.var(axis=1, keepdims=True) + 1e-5)
    z = f64(gamma) * hn
    return unpack_weight(w2_words, w2_scales).T @ mxq(z, 0, "e4m3")

@@ -1,0 +1,182 @@
+from contextlib import ExitStack
+
+import concourse.mybir as mybir
+
+K, T, S, H, N = 512, 4096, 1024, 512, 128
+FLOPS = 2 * K * H * S + 2 * H * N * S
+EPS = 1e-5
+
+F32 = mybir.dt.float32
+BF16 = mybir.dt.bfloat16
+I32 = mybir.dt.int32
+U32 = mybir.dt.uint32
+U16 = mybir.dt.uint16
+U8 = mybir.dt.uint8
+FP8X4 = mybir.dt.float8_e4m3fn_x4
+ACT = mybir.ActivationFunctionType
+ALU = mybir.AluOpType
+
+P = 128
+PACK = 4
+BANK = 512
+HALVES = S // BANK
+CHUNK = 256
+CHUNKS = S // CHUNK
+
+
+def tile_picked_inorm_none_p_kernel(
+    tc, x_words, x_scales, w1, w2_words, w2_scales, gamma, offs, out
+):
+    nc = tc.nc
+    with ExitStack() as ctx:
+        keep = ctx.enter_context(tc.tile_pool(name="keep", bufs=1))
+        psum = ctx.enter_context(tc.psum_pool(name="psum", bufs=1))
+
+        offsets = keep.tile([P, S // 16], U16, name="offsets")
+        nc.sync.dma_start(offsets[:], offs)
+
+        xs_all = keep.tile([P, T], U8, name="xs_all", align_bytes=64)
+        nc.sync.dma_start(xs_all[112:P, :].bitcast(I32), x_scales[0].bitcast(I32))
+        nc.vector.memset(xs_all[0:112, :].bitcast(I32), 0)
+
+        xw_all = keep.tile([P, T], U32, name="xw_all", align_bytes=64)
+        nc.sync.dma_start(
+            xw_all[:].bitcast(I32),
+            x_words[0].rearrange("p c r -> p (c r)").bitcast(I32),
+        )
+
+        w1_rows = w1.rearrange("(p j) c -> p j c", j=PACK)
+        w1_raw = []
+        for u in range(2):
+            raw = keep.tile([P, PACK, H // 2], F32, name="w1_raw%d" % u, align_bytes=64)
+            nc.sync.dma_start(raw[:], w1_rows[:, :, u * (H // 2) : (u + 1) * (H // 2)])
+            w1_raw.append(raw)
+
+        w2_codes = keep.tile([P, N], U32, name="w2_codes", align_bytes=64)
+        nc.sync.dma_start(
+            w2_codes[:].bitcast(I32),
+            w2_words[0].rearrange("p c r -> p (c r)").bitcast(I32),
+        )
+
+        xs = keep.tile([P, S], U8, name="xs", align_bytes=64)
+        nc.gpsimd.memset(xs[:].bitcast(I32), 0)
+        w2_sc = keep.tile([P, N], U8, name="w2_sc", align_bytes=64)
+        nc.gpsimd.memset(w2_sc[:].bitcast(I32), 0)
+        gam = keep.tile([P, PACK], F32, name="gam")
+        nc.gpsimd.dma_start(gam[:], gamma.rearrange("(p t) o -> p (t o)", t=PACK))
+        for q in range(4):
+            nc.gpsimd.dma_start(
+                w2_sc[32 * q : 32 * q + 4, :].bitcast(I32),
+                w2_scales[0][4 * q : 4 * q + 4, :].bitcast(I32),
+            )
+
+        xs_picked = keep.tile([P, S], U8, name="xs_picked", align_bytes=64)
+        nc.vector.tensor_copy(xs_picked[:], xs_all[:].indirect(offsets[:]))
+        for q in range(4):
+            nc.sync.dma_start(
+                xs[32 * q : 32 * q + 4, :].bitcast(I32),
+                xs_picked[112 + 4 * q : 116 + 4 * q, :].bitcast(I32),
+            )
+
+        mv = keep.tile([P, PACK, 4], F32, name="mv")
+        nc.vector.memset(mv[:], -1.0)
+
+        xw = keep.tile([P, S], U32, name="xw", align_bytes=64)
+        nc.vector.tensor_copy(xw[:], xw_all[:].indirect(offsets[:]))
+
+        w1_bf = keep.tile([P, PACK, P, PACK], BF16, name="w1_bf", align_bytes=64)
+        for u in range(2):
+            dst = w1_bf[:, :, u * (P // 2) : (u + 1) * (P // 2), :].rearrange("p t m j -> p m j t")
+            src = w1_raw[u][:].rearrange("p j (m t) -> p m j t", t=PACK)
+            if u == 0:
+                nc.scalar.copy(dst, src)
+            else:
+                nc.vector.tensor_copy(dst, src)
+
+        w1_codes = keep.tile([P, H], U32, name="w1_codes", align_bytes=64)
+        w1_sc = keep.tile([P, H], U8, name="w1_sc", align_bytes=64)
+        for t in range(PACK):
+            cols = slice(t * P, (t + 1) * P)
+            nc.vector.quantize_mx(
+                out=w1_codes[:, cols].bitcast(FP8X4),
+                scales=w1_sc[:, cols],
+                in_=w1_bf[:, t, :, :].rearrange("p m j -> p (m j)"),
+            )
+
+        h_ps = {}
+        for t in range(PACK):
+            cols = slice(t * P, (t + 1) * P)
+            for hf in range(HALVES):
+                toks = slice(hf * BANK, (hf + 1) * BANK)
+                bank = psum.tile([P, BANK], F32, name="h%d_%d" % (t, hf), tag="bank%d" % (t * HALVES + hf))
+                nc.tensor.matmul_mx(
+                    out=bank[:],
+                    lhsT=w1_codes[:, cols].bitcast(FP8X4),
+                    lhsT_scale=w1_sc[:, cols],
+                    rhs=xw[:, toks].bitcast(FP8X4),
+                    rhs_scale=xs[:, toks],
+                    start=True,
+                    stop=True,
+                )
+                h_ps[t, hf] = bank
+
+        planes = [
+            keep.tile([P, PACK, BANK], BF16, name="planes%d" % hf, align_bytes=64)
+            for hf in range(HALVES)
+        ]
+        for t in range(PACK):
+            stats = keep.tile([P, HALVES, 6], F32, name="stats%d" % t)
+            for hf in range(HALVES):
+                nc.vector.bn_stats(stats[:, hf, :], h_ps[t, hf][:])
+            nc.vector.bn_aggr(mv[:, t, 1:3], stats[:].rearrange("p a b -> p (a b)"))
+            gb = keep.tile([P, 2], F32, name="gb%d" % t)
+            nc.vector.tensor_scalar(
+                gb[:], mv[:, t, 0:2], gam[:, t : t + 1], -1.0, ALU.mult, ALU.mult
+            )
+            rstd = keep.tile([P, 1], F32, name="rstd%d" % t)
+            nc.scalar.activation(rstd[:], mv[:, t, 2:3], ACT.Abs_reciprocal_sqrt, bias=EPS)
+            ab = keep.tile([P, 2], F32, name="ab%d" % t)
+            nc.scalar.activation(ab[:], gb[:], ACT.Copy, scale=rstd[:])
+            for hf in range(HALVES):
+                if t == PACK - 1 and hf == 1:
+                    nc.vector.tensor_scalar(
+                        planes[hf][:, t, :], h_ps[t, hf][:], ab[:, 0:1], ab[:, 1:2], ALU.mult, ALU.add
+                    )
+                else:
+                    nc.scalar.activation(
+                        planes[hf][:, t, :], h_ps[t, hf][:], ACT.Identity, bias=ab[:, 1:2], scale=ab[:, 0:1]
+                    )
+
+        order = [2, 0, 3, 1]
+        z_bf = {}
+        for c in order:
+            hf, c0 = divmod(c * CHUNK, BANK)
+            zt = keep.tile([P, CHUNK, PACK], BF16, name="z_bf%d" % c, align_bytes=64)
+            dst = zt[:].rearrange("p (g i) t -> p g t i", i=4)
+            src = planes[hf][:, :, c0 : c0 + CHUNK].rearrange("p t (g i) -> p g t i", i=4)
+            if c == 0:
+                nc.scalar.copy(dst, src)
+            else:
+                nc.vector.tensor_copy(dst, src)
+            z_bf[c] = zt
+        for n, c in enumerate([2, 3, 0, 1]):
+            z_codes = keep.tile([P, CHUNK], U32, name="z_codes%d" % c, align_bytes=64)
+            z_sc = keep.tile([P, CHUNK], U8, name="z_sc%d" % c, align_bytes=64)
+            nc.vector.quantize_mx(
+                out=z_codes[:].bitcast(FP8X4),
+                scales=z_sc[:],
+                in_=z_bf[c][:].rearrange("p n t -> p (n t)"),
+            )
+            acc = psum.tile([P, BANK], F32, name="acc%d" % c, tag="bank%d" % n)
+            nc.tensor.matmul_mx(
+                out=acc[:, 0:CHUNK],
+                lhsT=w2_codes[:].bitcast(FP8X4),
+                lhsT_scale=w2_sc[:],
+                rhs=z_codes[:].bitcast(FP8X4),
+                rhs_scale=z_sc[:],
+                start=True,
+                stop=True,
+            )
+            res = keep.tile([P, CHUNK], F32, name="res%d" % c)
+            nc.scalar.copy(res[:], acc[:, 0:CHUNK])
+            nc.sync.dma_start(out[:, c * CHUNK : (c + 1) * CHUNK], res[:])

@@ -22,6 +22,9 @@ BANK = 512
 HALVES = S // BANK
 CHUNK = 256
 CHUNKS = S // CHUNK
+W1_FIRST = 224
+W1_VEC = 192
+S_TILE = 1
 
 
 def tile_picked_inorm_none_p_kernel(
@@ -35,6 +38,14 @@ def tile_picked_inorm_none_p_kernel(
         offsets = keep.tile([P, S // 16], U16, name="offsets")
         nc.sync.dma_start(offsets[:], offs)
 
+        mv = keep.tile([P, PACK, 4], F32, name="mv")
+        nc.vector.memset(mv[:], -1.0)
+        nc.vector.memset(mv[:, S_TILE, 0:1], -float(BANK))
+        rstd = keep.tile([P, PACK], F32, name="rstd")
+        nc.scalar.activation(rstd[:, 0:1], mv[:, 0, 0:1], ACT.Abs_reciprocal_sqrt, bias=EPS)
+        s_stats = keep.tile([P, HALVES, 3], F32, name="s_stats")
+        nc.vector.memset(s_stats[:], float(BANK))
+
         xs_all = keep.tile([P, T], U8, name="xs_all", align_bytes=64)
         nc.sync.dma_start(xs_all[112:P, :].bitcast(I32), x_scales[0].bitcast(I32))
         nc.vector.memset(xs_all[0:112, :].bitcast(I32), 0)
@@ -47,9 +58,9 @@ def tile_picked_inorm_none_p_kernel(
 
         w1_rows = w1.rearrange("(p j) c -> p j c", j=PACK)
         w1_raw = []
-        for u in range(2):
-            raw = keep.tile([P, PACK, H // 2], F32, name="w1_raw%d" % u, align_bytes=64)
-            nc.sync.dma_start(raw[:], w1_rows[:, :, u * (H // 2) : (u + 1) * (H // 2)])
+        for u, (lo, hi) in enumerate(((0, W1_FIRST), (W1_FIRST, H))):
+            raw = keep.tile([P, PACK, hi - lo], F32, name="w1_raw%d" % u, align_bytes=64)
+            nc.sync.dma_start(raw[:], w1_rows[:, :, lo:hi])
             w1_raw.append(raw)
 
         w2_codes = keep.tile([P, N], U32, name="w2_codes", align_bytes=64)
@@ -64,6 +75,8 @@ def tile_picked_inorm_none_p_kernel(
         nc.gpsimd.memset(w2_sc[:].bitcast(I32), 0)
         gam = keep.tile([P, PACK], F32, name="gam")
         nc.gpsimd.dma_start(gam[:], gamma.rearrange("(p t) o -> p (t o)", t=PACK))
+        neg_gam = keep.tile([P, PACK], F32, name="neg_gam")
+        nc.gpsimd.tensor_scalar(neg_gam[:], gam[:], -1.0, 1.0, ALU.mult, ALU.mult)
         for q in range(4):
             nc.gpsimd.dma_start(
                 w2_sc[32 * q : 32 * q + 4, :].bitcast(I32),
@@ -73,25 +86,42 @@ def tile_picked_inorm_none_p_kernel(
         xs_picked = keep.tile([P, S], U8, name="xs_picked", align_bytes=64)
         nc.vector.tensor_copy(xs_picked[:], xs_all[:].indirect(offsets[:]))
         for q in range(4):
-            nc.sync.dma_start(
+            nc.scalar.dma_start(
                 xs[32 * q : 32 * q + 4, :].bitcast(I32),
                 xs_picked[112 + 4 * q : 116 + 4 * q, :].bitcast(I32),
             )
 
-        mv = keep.tile([P, PACK, 4], F32, name="mv")
-        nc.vector.memset(mv[:], -1.0)
+        xw = []
+        for hf in range(HALVES):
+            picked = keep.tile([P, BANK], U32, name="xw%d" % hf, align_bytes=64)
+            cols = slice(hf * BANK // 16, (hf + 1) * BANK // 16)
+            nc.vector.tensor_copy(picked[:], xw_all[:].indirect(offsets[:, cols]))
+            xw.append(picked)
 
-        xw = keep.tile([P, S], U32, name="xw", align_bytes=64)
-        nc.vector.tensor_copy(xw[:], xw_all[:].indirect(offsets[:]))
+        warm = psum.tile([P, BANK], F32, name="warm", tag="bank7")
+        for width in (BANK, BANK, P):
+            nc.tensor.matmul_mx(
+                out=warm[:, 0:width],
+                lhsT=xw[0][:, 0:P].bitcast(FP8X4),
+                lhsT_scale=xs_picked[:, 0:P],
+                rhs=xw[0][:, 0:width].bitcast(FP8X4),
+                rhs_scale=xs_picked[:, 0:width],
+                start=True,
+                stop=True,
+            )
 
         w1_bf = keep.tile([P, PACK, P, PACK], BF16, name="w1_bf", align_bytes=64)
-        for u in range(2):
-            dst = w1_bf[:, :, u * (P // 2) : (u + 1) * (P // 2), :].rearrange("p t m j -> p m j t")
-            src = w1_raw[u][:].rearrange("p j (m t) -> p m j t", t=PACK)
-            if u == 0:
-                nc.scalar.copy(dst, src)
-            else:
-                nc.vector.tensor_copy(dst, src)
+        shares = (
+            (nc.scalar.copy, 0, 0, W1_FIRST),
+            (nc.vector.tensor_copy, 1, W1_FIRST, W1_FIRST + W1_VEC),
+            (nc.scalar.copy, 1, W1_FIRST + W1_VEC, H),
+        )
+        for copy, u, lo, hi in shares:
+            base = u * W1_FIRST
+            copy(
+                w1_bf[:, :, lo // PACK : hi // PACK, :].rearrange("p t m j -> p m j t"),
+                w1_raw[u][:, :, lo - base : hi - base].rearrange("p j (m t) -> p m j t", t=PACK),
+            )
 
         w1_codes = keep.tile([P, H], U32, name="w1_codes", align_bytes=64)
         w1_sc = keep.tile([P, H], U8, name="w1_sc", align_bytes=64)
@@ -104,16 +134,16 @@ def tile_picked_inorm_none_p_kernel(
             )
 
         h_ps = {}
-        for t in range(PACK):
+        for t, hf in ((0, 0), (1, 0), (0, 1), (1, 1), (2, 0), (2, 1), (3, 0), (3, 1)):
             cols = slice(t * P, (t + 1) * P)
-            for hf in range(HALVES):
+            if True:
                 toks = slice(hf * BANK, (hf + 1) * BANK)
                 bank = psum.tile([P, BANK], F32, name="h%d_%d" % (t, hf), tag="bank%d" % (t * HALVES + hf))
                 nc.tensor.matmul_mx(
                     out=bank[:],
                     lhsT=w1_codes[:, cols].bitcast(FP8X4),
                     lhsT_scale=w1_sc[:, cols],
-                    rhs=xw[:, toks].bitcast(FP8X4),
+                    rhs=xw[hf][:].bitcast(FP8X4),
                     rhs_scale=xs[:, toks],
                     start=True,
                     stop=True,
@@ -124,52 +154,85 @@ def tile_picked_inorm_none_p_kernel(
             keep.tile([P, PACK, BANK], BF16, name="planes%d" % hf, align_bytes=64)
             for hf in range(HALVES)
         ]
-        for t in range(PACK):
-            stats = keep.tile([P, HALVES, 6], F32, name="stats%d" % t)
-            for hf in range(HALVES):
-                nc.vector.bn_stats(stats[:, hf, :], h_ps[t, hf][:])
-            nc.vector.bn_aggr(mv[:, t, 1:3], stats[:].rearrange("p a b -> p (a b)"))
-            gb = keep.tile([P, 2], F32, name="gb%d" % t)
-            nc.vector.tensor_scalar(
-                gb[:], mv[:, t, 0:2], gam[:, t : t + 1], -1.0, ALU.mult, ALU.mult
-            )
-            rstd = keep.tile([P, 1], F32, name="rstd%d" % t)
-            nc.scalar.activation(rstd[:], mv[:, t, 2:3], ACT.Abs_reciprocal_sqrt, bias=EPS)
-            ab = keep.tile([P, 2], F32, name="ab%d" % t)
-            nc.scalar.activation(ab[:], gb[:], ACT.Copy, scale=rstd[:])
-            for hf in range(HALVES):
-                if t == PACK - 1 and hf == 1:
-                    nc.vector.tensor_scalar(
-                        planes[hf][:, t, :], h_ps[t, hf][:], ab[:, 0:1], ab[:, 1:2], ALU.mult, ALU.add
-                    )
-                else:
-                    nc.scalar.activation(
-                        planes[hf][:, t, :], h_ps[t, hf][:], ACT.Identity, bias=ab[:, 1:2], scale=ab[:, 0:1]
-                    )
+        coef = {}
 
-        order = [2, 0, 3, 1]
-        z_bf = {}
-        for c in order:
-            hf, c0 = divmod(c * CHUNK, BANK)
-            zt = keep.tile([P, CHUNK, PACK], BF16, name="z_bf%d" % c, align_bytes=64)
-            dst = zt[:].rearrange("p (g i) t -> p g t i", i=4)
-            src = planes[hf][:, :, c0 : c0 + CHUNK].rearrange("p t (g i) -> p g t i", i=4)
-            if c == 0:
-                nc.scalar.copy(dst, src)
+        def norm_scalar(t, hf, lo, hi):
+            nc.scalar.activation(
+                planes[hf][:, t, lo:hi], h_ps[t, hf][:, lo:hi], ACT.Identity,
+                bias=coef[t][:, 1:2], scale=coef[t][:, 0:1],
+            )
+
+        def norm_vector(t, hf, lo, hi):
+            nc.vector.tensor_scalar(
+                planes[hf][:, t, lo:hi], h_ps[t, hf][:, lo:hi],
+                coef[t][:, 0:1], coef[t][:, 1:2], ALU.mult, ALU.add,
+            )
+
+        h_sb = keep.tile([P, HALVES, BANK], F32, name="h_sb", align_bytes=64)
+        for hf in range(HALVES):
+            nc.scalar.activation(
+                h_sb[:, hf, :], h_ps[S_TILE, hf][:], ACT.Copy, scale=1.0 / BANK,
+                accum_out=s_stats[:, hf, 1:2],
+            )
+        def squares(hf):
+            nc.scalar.activation(
+                planes[hf][:, S_TILE, :], h_ps[S_TILE, hf][:], ACT.Square, scale=-1.0,
+                bias=s_stats[:, hf, 1:2], accum_out=s_stats[:, hf, 2:3],
+            )
+
+        squares(0)
+        for t in (0, 1, 2, 3):
+            if t == S_TILE:
+                squares(1)
+                stats = s_stats
             else:
-                nc.vector.tensor_copy(dst, src)
-            z_bf[c] = zt
-        for n, c in enumerate([2, 3, 0, 1]):
-            z_codes = keep.tile([P, CHUNK], U32, name="z_codes%d" % c, align_bytes=64)
-            z_sc = keep.tile([P, CHUNK], U8, name="z_sc%d" % c, align_bytes=64)
+                stats = keep.tile([P, HALVES, 6], F32, name="stats%d" % t)
+                for hf in range(HALVES):
+                    nc.vector.bn_stats(stats[:, hf, :], h_ps[t, hf][:])
+            nc.vector.bn_aggr(mv[:, t, 1:3], stats[:].rearrange("p a b -> p (a b)"))
+            nc.scalar.activation(rstd[:, t : t + 1], mv[:, t, 2:3], ACT.Abs_reciprocal_sqrt, bias=EPS)
+            ab = keep.tile([P, 2], F32, name="ab%d" % t)
+            nc.vector.tensor_scalar(
+                ab[:], mv[:, t, 0:2], rstd[:, t : t + 1], neg_gam[:, t : t + 1], ALU.mult, ALU.mult
+            )
+            coef[t] = ab
+
+        norm_scalar(0, 0, 0, BANK)
+        norm_scalar(0, 1, 0, BANK)
+        norm_scalar(2, 0, 0, BANK)
+        for hf in range(HALVES):
+            nc.vector.tensor_scalar(
+                planes[hf][:, S_TILE, :], h_sb[:, hf, :],
+                coef[S_TILE][:, 0:1], coef[S_TILE][:, 1:2], ALU.mult, ALU.add,
+            )
+        norm_vector(3, 0, 0, BANK)
+        norm_scalar(2, 1, 0, BANK)
+        norm_scalar(3, 1, 0, BANK)
+
+        pieces = ((0, 256), (256, 512), (512, 768), (768, 896), (896, 1024))
+        z_bf = {}
+
+        def weave(copy, c):
+            lo, hi = pieces[c]
+            hf, c0 = divmod(lo, BANK)
+            z_bf[c] = keep.tile([P, hi - lo, PACK], BF16, name="z_bf%d" % c, align_bytes=64)
+            copy(
+                z_bf[c][:].rearrange("p (g i) t -> p g t i", i=4),
+                planes[hf][:, :, c0 : c0 + hi - lo].rearrange("p t (g i) -> p g t i", i=4),
+            )
+
+        def finish(c, evac):
+            lo, hi = pieces[c]
+            z_codes = keep.tile([P, hi - lo], U32, name="z_codes%d" % c, align_bytes=64)
+            z_sc = keep.tile([P, hi - lo], U8, name="z_sc%d" % c, align_bytes=64)
             nc.vector.quantize_mx(
                 out=z_codes[:].bitcast(FP8X4),
                 scales=z_sc[:],
                 in_=z_bf[c][:].rearrange("p n t -> p (n t)"),
             )
-            acc = psum.tile([P, BANK], F32, name="acc%d" % c, tag="bank%d" % n)
+            acc = psum.tile([P, BANK], F32, name="acc%d" % c, tag="bank%d" % c)
             nc.tensor.matmul_mx(
-                out=acc[:, 0:CHUNK],
+                out=acc[:, 0 : hi - lo],
                 lhsT=w2_codes[:].bitcast(FP8X4),
                 lhsT_scale=w2_sc[:],
                 rhs=z_codes[:].bitcast(FP8X4),
@@ -177,6 +240,17 @@ def tile_picked_inorm_none_p_kernel(
                 start=True,
                 stop=True,
             )
-            res = keep.tile([P, CHUNK], F32, name="res%d" % c)
-            nc.scalar.copy(res[:], acc[:, 0:CHUNK])
-            nc.sync.dma_start(out[:, c * CHUNK : (c + 1) * CHUNK], res[:])
+            res = keep.tile([P, hi - lo], F32, name="res%d" % c)
+            evac(res[:], acc[:, 0 : hi - lo])
+            nc.sync.dma_start(out[:, lo:hi], res[:])
+
+        weave(nc.vector.tensor_copy, 0)
+        weave(nc.vector.tensor_copy, 1)
+        weave(nc.scalar.copy, 2)
+        weave(nc.scalar.copy, 3)
+        finish(0, nc.scalar.copy)
+        finish(1, nc.scalar.copy)
+        weave(nc.vector.tensor_copy, 4)
+        finish(2, nc.scalar.copy)
+        finish(4, nc.vector.tensor_copy)
+        finish(3, nc.vector.tensor_copy)

@@ -50,6 +50,11 @@ def tile_picked_inorm_none_p_kernel(
         nc.sync.dma_start(xs_all[112:P, :].bitcast(I32), x_scales[0].bitcast(I32))
         nc.vector.memset(xs_all[0:112, :].bitcast(I32), 0)
 
+        gam = keep.tile([P, PACK], F32, name="gam")
+        nc.sync.dma_start(gam[:], gamma.rearrange("(p t) o -> p (t o)", t=PACK))
+        neg_gam = keep.tile([P, PACK], F32, name="neg_gam")
+        nc.scalar.activation(neg_gam[:], gam[:], ACT.Copy, scale=-1.0)
+
         xw_all = keep.tile([P, T], U32, name="xw_all", align_bytes=64)
         nc.sync.dma_start(
             xw_all[:].bitcast(I32),
@@ -59,29 +64,12 @@ def tile_picked_inorm_none_p_kernel(
         w1_rows = w1.rearrange("(p j) c -> p j c", j=PACK)
         w1_raw = []
         for u, (lo, hi) in enumerate(((0, W1_FIRST), (W1_FIRST, H))):
-            raw = keep.tile([P, PACK, hi - lo], F32, name="w1_raw%d" % u, align_bytes=64)
+            raw = keep.tile([P, PACK, hi - lo], F32, name="w1_raw%d" % u, tag="w1_raw%d" % u, align_bytes=64)
             nc.sync.dma_start(raw[:], w1_rows[:, :, lo:hi])
             w1_raw.append(raw)
 
-        w2_codes = keep.tile([P, N], U32, name="w2_codes", align_bytes=64)
-        nc.sync.dma_start(
-            w2_codes[:].bitcast(I32),
-            w2_words[0].rearrange("p c r -> p (c r)").bitcast(I32),
-        )
-
         xs = keep.tile([P, S], U8, name="xs", align_bytes=64)
         nc.gpsimd.memset(xs[:].bitcast(I32), 0)
-        w2_sc = keep.tile([P, N], U8, name="w2_sc", align_bytes=64)
-        nc.gpsimd.memset(w2_sc[:].bitcast(I32), 0)
-        gam = keep.tile([P, PACK], F32, name="gam")
-        nc.gpsimd.dma_start(gam[:], gamma.rearrange("(p t) o -> p (t o)", t=PACK))
-        neg_gam = keep.tile([P, PACK], F32, name="neg_gam")
-        nc.gpsimd.tensor_scalar(neg_gam[:], gam[:], -1.0, 1.0, ALU.mult, ALU.mult)
-        for q in range(4):
-            nc.gpsimd.dma_start(
-                w2_sc[32 * q : 32 * q + 4, :].bitcast(I32),
-                w2_scales[0][4 * q : 4 * q + 4, :].bitcast(I32),
-            )
 
         xs_picked = keep.tile([P, S], U8, name="xs_picked", align_bytes=64)
         nc.vector.tensor_copy(xs_picked[:], xs_all[:].indirect(offsets[:]))
@@ -99,7 +87,7 @@ def tile_picked_inorm_none_p_kernel(
             xw.append(picked)
 
         warm = psum.tile([P, BANK], F32, name="warm", tag="bank7")
-        for width in (BANK, BANK, P):
+        for width in (BANK, BANK, BANK // 2):
             nc.tensor.matmul_mx(
                 out=warm[:, 0:width],
                 lhsT=xw[0][:, 0:P].bitcast(FP8X4),
@@ -123,14 +111,27 @@ def tile_picked_inorm_none_p_kernel(
                 w1_raw[u][:, :, lo - base : hi - base].rearrange("p j (m t) -> p m j t", t=PACK),
             )
 
+        w2_sc = keep.tile([P, N], U8, name="w2_sc", tag="w1_raw0", align_bytes=64)
+        nc.gpsimd.memset(w2_sc[:].bitcast(I32), 0)
+        for q in range(4):
+            nc.sync.dma_start(
+                w2_sc[32 * q : 32 * q + 4, :].bitcast(I32),
+                w2_scales[0][4 * q : 4 * q + 4, :].bitcast(I32),
+            )
+        w2_codes = keep.tile([P, N], U32, name="w2_codes", tag="w1_raw1", align_bytes=64)
+        nc.sync.dma_start(
+            w2_codes[:].bitcast(I32),
+            w2_words[0].rearrange("p c r -> p (c r)").bitcast(I32),
+        )
+
         w1_codes = keep.tile([P, H], U32, name="w1_codes", align_bytes=64)
         w1_sc = keep.tile([P, H], U8, name="w1_sc", align_bytes=64)
-        for t in range(PACK):
-            cols = slice(t * P, (t + 1) * P)
+        for lo, hi in ((0, 1), (1, 2), (2, 4)):
+            cols = slice(lo * P, hi * P)
             nc.vector.quantize_mx(
                 out=w1_codes[:, cols].bitcast(FP8X4),
                 scales=w1_sc[:, cols],
-                in_=w1_bf[:, t, :, :].rearrange("p m j -> p (m j)"),
+                in_=w1_bf[:, lo:hi, :, :].rearrange("p t m j -> p (t m j)"),
             )
 
         h_ps = {}
@@ -205,7 +206,8 @@ def tile_picked_inorm_none_p_kernel(
                 planes[hf][:, S_TILE, :], h_sb[:, hf, :],
                 coef[S_TILE][:, 0:1], coef[S_TILE][:, 1:2], ALU.mult, ALU.add,
             )
-        norm_vector(3, 0, 0, BANK)
+        norm_vector(3, 0, 0, CHUNK)
+        norm_scalar(3, 0, CHUNK, BANK)
         norm_scalar(2, 1, 0, BANK)
         norm_scalar(3, 1, 0, BANK)
 
@@ -247,10 +249,10 @@ def tile_picked_inorm_none_p_kernel(
         weave(nc.vector.tensor_copy, 0)
         weave(nc.vector.tensor_copy, 1)
         weave(nc.scalar.copy, 2)
-        weave(nc.scalar.copy, 3)
         finish(0, nc.scalar.copy)
         finish(1, nc.scalar.copy)
+        weave(nc.vector.tensor_copy, 3)
         weave(nc.vector.tensor_copy, 4)
         finish(2, nc.scalar.copy)
+        finish(3, nc.scalar.copy)
         finish(4, nc.vector.tensor_copy)
-        finish(3, nc.vector.tensor_copy)

@@ -22,8 +22,8 @@ BANK = 512
 HALVES = S // BANK
 CHUNK = 256
 CHUNKS = S // CHUNK
-W1_FIRST = 224
-W1_VEC = 192
+X_FIRST = 1536
+W1_VEC = 344
 S_TILE = 1
 
 
@@ -36,7 +36,9 @@ def tile_picked_inorm_none_p_kernel(
         psum = ctx.enter_context(tc.psum_pool(name="psum", bufs=1))
 
         offsets = keep.tile([P, S // 16], U16, name="offsets")
-        nc.sync.dma_start(offsets[:], offs)
+
+        xs_all = keep.tile([P, T], U8, name="xs_all", tag="xs_all", align_bytes=64)
+        nc.vector.memset(xs_all[:].bitcast(I32), 0)
 
         mv = keep.tile([P, PACK, 4], F32, name="mv")
         nc.vector.memset(mv[:], -1.0)
@@ -46,27 +48,20 @@ def tile_picked_inorm_none_p_kernel(
         s_stats = keep.tile([P, HALVES, 3], F32, name="s_stats")
         nc.vector.memset(s_stats[:], float(BANK))
 
-        xs_all = keep.tile([P, T], U8, name="xs_all", align_bytes=64)
-        nc.sync.dma_start(xs_all[112:P, :].bitcast(I32), x_scales[0].bitcast(I32))
-        nc.vector.memset(xs_all[0:112, :].bitcast(I32), 0)
+
+        xw_all = keep.tile([P, T], U32, name="xw_all", align_bytes=64)
+        x_rows = x_words[0].rearrange("p c r -> p (c r)").bitcast(I32)
+        nc.sync.dma_start(xw_all[:, 0:X_FIRST].bitcast(I32), x_rows[:, 0:X_FIRST])
+        nc.sync.dma_start(offsets[:], offs)
+        nc.sync.dma_start(xs_all[0:P:8, :].bitcast(I32), x_scales[0].bitcast(I32))
+        nc.sync.dma_start(xw_all[:, X_FIRST:T].bitcast(I32), x_rows[:, X_FIRST:T])
+
+        w1_rows = w1.rearrange("(p j) c -> p j c", j=PACK)
+        w1_raw = keep.tile([P, PACK, H], F32, name="w1_raw", tag="w1_raw", align_bytes=64)
+        nc.sync.dma_start(w1_raw[:], w1_rows)
 
         gam = keep.tile([P, PACK], F32, name="gam")
         nc.sync.dma_start(gam[:], gamma.rearrange("(p t) o -> p (t o)", t=PACK))
-        neg_gam = keep.tile([P, PACK], F32, name="neg_gam")
-        nc.scalar.activation(neg_gam[:], gam[:], ACT.Copy, scale=-1.0)
-
-        xw_all = keep.tile([P, T], U32, name="xw_all", align_bytes=64)
-        nc.sync.dma_start(
-            xw_all[:].bitcast(I32),
-            x_words[0].rearrange("p c r -> p (c r)").bitcast(I32),
-        )
-
-        w1_rows = w1.rearrange("(p j) c -> p j c", j=PACK)
-        w1_raw = []
-        for u, (lo, hi) in enumerate(((0, W1_FIRST), (W1_FIRST, H))):
-            raw = keep.tile([P, PACK, hi - lo], F32, name="w1_raw%d" % u, tag="w1_raw%d" % u, align_bytes=64)
-            nc.sync.dma_start(raw[:], w1_rows[:, :, lo:hi])
-            w1_raw.append(raw)
 
         xs = keep.tile([P, S], U8, name="xs", align_bytes=64)
         nc.gpsimd.memset(xs[:].bitcast(I32), 0)
@@ -76,7 +71,7 @@ def tile_picked_inorm_none_p_kernel(
         for q in range(4):
             nc.scalar.dma_start(
                 xs[32 * q : 32 * q + 4, :].bitcast(I32),
-                xs_picked[112 + 4 * q : 116 + 4 * q, :].bitcast(I32),
+                xs_picked[32 * q : 32 * q + 32 : 8, :].bitcast(I32),
             )
 
         xw = []
@@ -99,26 +94,22 @@ def tile_picked_inorm_none_p_kernel(
             )
 
         w1_bf = keep.tile([P, PACK, P, PACK], BF16, name="w1_bf", align_bytes=64)
-        shares = (
-            (nc.scalar.copy, 0, 0, W1_FIRST),
-            (nc.vector.tensor_copy, 1, W1_FIRST, W1_FIRST + W1_VEC),
-            (nc.scalar.copy, 1, W1_FIRST + W1_VEC, H),
-        )
-        for copy, u, lo, hi in shares:
-            base = u * W1_FIRST
+        for copy, lo, hi in ((nc.vector.tensor_copy, 0, W1_VEC), (nc.scalar.copy, W1_VEC, H)):
             copy(
                 w1_bf[:, :, lo // PACK : hi // PACK, :].rearrange("p t m j -> p m j t"),
-                w1_raw[u][:, :, lo - base : hi - base].rearrange("p j (m t) -> p m j t", t=PACK),
+                w1_raw[:, :, lo:hi].rearrange("p j (m t) -> p m j t", t=PACK),
             )
+        neg_gam = keep.tile([P, PACK], F32, name="neg_gam")
+        nc.scalar.activation(neg_gam[:], gam[:], ACT.Copy, scale=-1.0)
 
-        w2_sc = keep.tile([P, N], U8, name="w2_sc", tag="w1_raw0", align_bytes=64)
+        w2_sc = keep.tile([P, N], U8, name="w2_sc", tag="xs_all", align_bytes=64)
         nc.gpsimd.memset(w2_sc[:].bitcast(I32), 0)
         for q in range(4):
             nc.sync.dma_start(
                 w2_sc[32 * q : 32 * q + 4, :].bitcast(I32),
                 w2_scales[0][4 * q : 4 * q + 4, :].bitcast(I32),
             )
-        w2_codes = keep.tile([P, N], U32, name="w2_codes", tag="w1_raw1", align_bytes=64)
+        w2_codes = keep.tile([P, N], U32, name="w2_codes", tag="w1_raw", align_bytes=64)
         nc.sync.dma_start(
             w2_codes[:].bitcast(I32),
             w2_words[0].rearrange("p c r -> p (c r)").bitcast(I32),

@@ -23,8 +23,9 @@ HALVES = S // BANK
 CHUNK = 256
 CHUNKS = S // CHUNK
 X_FIRST = 1536
-W1_VEC = 344
+W1_VEC = 76
 S_TILE = 1
+PASS = 128
 
 
 def tile_picked_inorm_none_p_kernel(
@@ -94,11 +95,32 @@ def tile_picked_inorm_none_p_kernel(
             )
 
         w1_bf = keep.tile([P, PACK, P, PACK], BF16, name="w1_bf", align_bytes=64)
-        for copy, lo, hi in ((nc.vector.tensor_copy, 0, W1_VEC), (nc.scalar.copy, W1_VEC, H)):
+        w1_codes = keep.tile([P, H], U32, name="w1_codes", align_bytes=64)
+        w1_sc = keep.tile([P, H], U8, name="w1_sc", align_bytes=64)
+        w1_deal = w1_raw[:].rearrange("p j (m t) -> p m j t", t=PACK)
+
+        def cast(copy, pair, lo, hi):
             copy(
-                w1_bf[:, :, lo // PACK : hi // PACK, :].rearrange("p t m j -> p m j t"),
-                w1_raw[:, :, lo:hi].rearrange("p j (m t) -> p m j t", t=PACK),
+                w1_bf[:, 2 * pair : 2 * pair + 2, lo:hi, :].rearrange("p t m j -> p m j t"),
+                w1_deal[:, lo:hi, :, 2 * pair : 2 * pair + 2],
             )
+
+        def quantise_w1(lo, hi):
+            cols = slice(lo * P, hi * P)
+            nc.vector.quantize_mx(
+                out=w1_codes[:, cols].bitcast(FP8X4),
+                scales=w1_sc[:, cols],
+                in_=w1_bf[:, lo:hi, :, :].rearrange("p t m j -> p (t m j)"),
+            )
+
+        cast(nc.vector.tensor_copy, 0, 0, W1_VEC)
+        cast(nc.scalar.copy, 0, W1_VEC, P)
+        cast(nc.scalar.copy, 1, W1_VEC, P)
+        cast(nc.vector.tensor_copy, 1, 0, W1_VEC // 2)
+        quantise_w1(1, 2)
+        quantise_w1(0, 1)
+        cast(nc.vector.tensor_copy, 1, W1_VEC // 2, W1_VEC)
+        quantise_w1(2, 4)
         neg_gam = keep.tile([P, PACK], F32, name="neg_gam")
         nc.scalar.activation(neg_gam[:], gam[:], ACT.Copy, scale=-1.0)
 
@@ -115,32 +137,21 @@ def tile_picked_inorm_none_p_kernel(
             w2_words[0].rearrange("p c r -> p (c r)").bitcast(I32),
         )
 
-        w1_codes = keep.tile([P, H], U32, name="w1_codes", align_bytes=64)
-        w1_sc = keep.tile([P, H], U8, name="w1_sc", align_bytes=64)
-        for lo, hi in ((0, 1), (1, 2), (2, 4)):
-            cols = slice(lo * P, hi * P)
-            nc.vector.quantize_mx(
-                out=w1_codes[:, cols].bitcast(FP8X4),
-                scales=w1_sc[:, cols],
-                in_=w1_bf[:, lo:hi, :, :].rearrange("p t m j -> p (t m j)"),
-            )
-
         h_ps = {}
-        for t, hf in ((0, 0), (1, 0), (0, 1), (1, 1), (2, 0), (2, 1), (3, 0), (3, 1)):
+        for t, hf in ((1, 0), (0, 0), (1, 1), (0, 1), (2, 0), (2, 1), (3, 0), (3, 1)):
             cols = slice(t * P, (t + 1) * P)
-            if True:
-                toks = slice(hf * BANK, (hf + 1) * BANK)
-                bank = psum.tile([P, BANK], F32, name="h%d_%d" % (t, hf), tag="bank%d" % (t * HALVES + hf))
+            bank = psum.tile([P, BANK], F32, name="h%d_%d" % (t, hf), tag="bank%d" % (t * HALVES + hf))
+            for lo in range(0, BANK, PASS):
                 nc.tensor.matmul_mx(
-                    out=bank[:],
+                    out=bank[:, lo : lo + PASS],
                     lhsT=w1_codes[:, cols].bitcast(FP8X4),
                     lhsT_scale=w1_sc[:, cols],
-                    rhs=xw[hf][:].bitcast(FP8X4),
-                    rhs_scale=xs[:, toks],
+                    rhs=xw[hf][:, lo : lo + PASS].bitcast(FP8X4),
+                    rhs_scale=xs[:, hf * BANK + lo : hf * BANK + lo + PASS],
                     start=True,
                     stop=True,
                 )
-                h_ps[t, hf] = bank
+            h_ps[t, hf] = bank
 
         planes = [
             keep.tile([P, PACK, BANK], BF16, name="planes%d" % hf, align_bytes=64)

@@ -20,12 +20,12 @@ P = 128
 PACK = 4
 BANK = 512
 HALVES = S // BANK
-CHUNK = 256
-CHUNKS = S // CHUNK
-X_FIRST = 1536
-W1_VEC = 76
-S_TILE = 1
 PASS = 128
+X_FIRST = 1536
+ROW0, ROW_STEP = 11, 7
+W1_VECTOR = 76
+SCALAR_TILE = 1
+PIECES = ((0, 256), (256, 512), (512, 768), (768, 896), (896, 1024))
 
 
 def tile_picked_inorm_none_p_kernel(
@@ -42,24 +42,25 @@ def tile_picked_inorm_none_p_kernel(
         nc.vector.memset(xs_all[:].bitcast(I32), 0)
 
         mv = keep.tile([P, PACK, 4], F32, name="mv")
-        nc.vector.memset(mv[:], -1.0)
-        nc.vector.memset(mv[:, S_TILE, 0:1], -float(BANK))
+        nc.vector.memset(mv[:, :, 0:1], -1.0)
+        nc.vector.memset(mv[:, SCALAR_TILE, 0:1], -float(BANK))
         rstd = keep.tile([P, PACK], F32, name="rstd")
         nc.scalar.activation(rstd[:, 0:1], mv[:, 0, 0:1], ACT.Abs_reciprocal_sqrt, bias=EPS)
         s_stats = keep.tile([P, HALVES, 3], F32, name="s_stats")
-        nc.vector.memset(s_stats[:], float(BANK))
-
+        nc.vector.memset(s_stats[:, :, 0:1], float(BANK))
 
         xw_all = keep.tile([P, T], U32, name="xw_all", align_bytes=64)
         x_rows = x_words[0].rearrange("p c r -> p (c r)").bitcast(I32)
         nc.sync.dma_start(xw_all[:, 0:X_FIRST].bitcast(I32), x_rows[:, 0:X_FIRST])
         nc.sync.dma_start(offsets[:], offs)
-        nc.sync.dma_start(xs_all[0:P:8, :].bitcast(I32), x_scales[0].bitcast(I32))
+        nc.sync.dma_start(
+            xs_all[ROW0 : ROW0 + 15 * ROW_STEP + 1 : ROW_STEP, :].bitcast(I32),
+            x_scales[0].bitcast(I32),
+        )
         nc.sync.dma_start(xw_all[:, X_FIRST:T].bitcast(I32), x_rows[:, X_FIRST:T])
 
-        w1_rows = w1.rearrange("(p j) c -> p j c", j=PACK)
         w1_raw = keep.tile([P, PACK, H], F32, name="w1_raw", tag="w1_raw", align_bytes=64)
-        nc.sync.dma_start(w1_raw[:], w1_rows)
+        nc.sync.dma_start(w1_raw[:], w1.rearrange("(p j) c -> p j c", j=PACK))
 
         gam = keep.tile([P, PACK], F32, name="gam")
         nc.sync.dma_start(gam[:], gamma.rearrange("(p t) o -> p (t o)", t=PACK))
@@ -70,16 +71,17 @@ def tile_picked_inorm_none_p_kernel(
         xs_picked = keep.tile([P, S], U8, name="xs_picked", align_bytes=64)
         nc.vector.tensor_copy(xs_picked[:], xs_all[:].indirect(offsets[:]))
         for q in range(4):
+            first = ROW0 + 4 * q * ROW_STEP
             nc.scalar.dma_start(
                 xs[32 * q : 32 * q + 4, :].bitcast(I32),
-                xs_picked[32 * q : 32 * q + 32 : 8, :].bitcast(I32),
+                xs_picked[first : first + 3 * ROW_STEP + 1 : ROW_STEP, :].bitcast(I32),
             )
 
         xw = []
         for hf in range(HALVES):
             picked = keep.tile([P, BANK], U32, name="xw%d" % hf, align_bytes=64)
-            cols = slice(hf * BANK // 16, (hf + 1) * BANK // 16)
-            nc.vector.tensor_copy(picked[:], xw_all[:].indirect(offsets[:, cols]))
+            entries = slice(hf * BANK // 16, (hf + 1) * BANK // 16)
+            nc.vector.tensor_copy(picked[:], xw_all[:].indirect(offsets[:, entries]))
             xw.append(picked)
 
         warm = psum.tile([P, BANK], F32, name="warm", tag="bank7")
@@ -97,29 +99,29 @@ def tile_picked_inorm_none_p_kernel(
         w1_bf = keep.tile([P, PACK, P, PACK], BF16, name="w1_bf", align_bytes=64)
         w1_codes = keep.tile([P, H], U32, name="w1_codes", align_bytes=64)
         w1_sc = keep.tile([P, H], U8, name="w1_sc", align_bytes=64)
-        w1_deal = w1_raw[:].rearrange("p j (m t) -> p m j t", t=PACK)
+        w1_dealt = w1_raw[:].rearrange("p j (m t) -> p m j t", t=PACK)
 
-        def cast(copy, pair, lo, hi):
+        def round_w1(copy, pair, lo, hi):
             copy(
                 w1_bf[:, 2 * pair : 2 * pair + 2, lo:hi, :].rearrange("p t m j -> p m j t"),
-                w1_deal[:, lo:hi, :, 2 * pair : 2 * pair + 2],
+                w1_dealt[:, lo:hi, :, 2 * pair : 2 * pair + 2],
             )
 
-        def quantise_w1(lo, hi):
-            cols = slice(lo * P, hi * P)
+        def quantise_w1(first_tile, end_tile):
+            cols = slice(first_tile * P, end_tile * P)
             nc.vector.quantize_mx(
                 out=w1_codes[:, cols].bitcast(FP8X4),
                 scales=w1_sc[:, cols],
-                in_=w1_bf[:, lo:hi, :, :].rearrange("p t m j -> p (t m j)"),
+                in_=w1_bf[:, first_tile:end_tile, :, :].rearrange("p t m j -> p (t m j)"),
             )
 
-        cast(nc.vector.tensor_copy, 0, 0, W1_VEC)
-        cast(nc.scalar.copy, 0, W1_VEC, P)
-        cast(nc.scalar.copy, 1, W1_VEC, P)
-        cast(nc.vector.tensor_copy, 1, 0, W1_VEC // 2)
+        round_w1(nc.vector.tensor_copy, 0, 0, W1_VECTOR)
+        round_w1(nc.scalar.copy, 0, W1_VECTOR, P)
+        round_w1(nc.scalar.copy, 1, W1_VECTOR, P)
+        round_w1(nc.vector.tensor_copy, 1, 0, W1_VECTOR // 2)
         quantise_w1(1, 2)
         quantise_w1(0, 1)
-        cast(nc.vector.tensor_copy, 1, W1_VEC // 2, W1_VEC)
+        round_w1(nc.vector.tensor_copy, 1, W1_VECTOR // 2, W1_VECTOR)
         quantise_w1(2, 4)
         neg_gam = keep.tile([P, PACK], F32, name="neg_gam")
         nc.scalar.activation(neg_gam[:], gam[:], ACT.Copy, scale=-1.0)
@@ -153,7 +155,7 @@ def tile_picked_inorm_none_p_kernel(
                 )
             h_ps[t, hf] = bank
 
-        planes = [
+        z_tiles = [
             keep.tile([P, PACK, BANK], BF16, name="planes%d" % hf, align_bytes=64)
             for hf in range(HALVES)
         ]
@@ -161,32 +163,33 @@ def tile_picked_inorm_none_p_kernel(
 
         def norm_scalar(t, hf, lo, hi):
             nc.scalar.activation(
-                planes[hf][:, t, lo:hi], h_ps[t, hf][:, lo:hi], ACT.Identity,
+                z_tiles[hf][:, t, lo:hi], h_ps[t, hf][:, lo:hi], ACT.Identity,
                 bias=coef[t][:, 1:2], scale=coef[t][:, 0:1],
             )
 
-        def norm_vector(t, hf, lo, hi):
+        def norm_vector(t, hf, lo, hi, source):
             nc.vector.tensor_scalar(
-                planes[hf][:, t, lo:hi], h_ps[t, hf][:, lo:hi],
+                z_tiles[hf][:, t, lo:hi], source,
                 coef[t][:, 0:1], coef[t][:, 1:2], ALU.mult, ALU.add,
             )
 
         h_sb = keep.tile([P, HALVES, BANK], F32, name="h_sb", align_bytes=64)
         for hf in range(HALVES):
             nc.scalar.activation(
-                h_sb[:, hf, :], h_ps[S_TILE, hf][:], ACT.Copy, scale=1.0 / BANK,
+                h_sb[:, hf, :], h_ps[SCALAR_TILE, hf][:], ACT.Copy, scale=1.0 / BANK,
                 accum_out=s_stats[:, hf, 1:2],
             )
-        def squares(hf):
+
+        def centred_squares(hf):
             nc.scalar.activation(
-                planes[hf][:, S_TILE, :], h_ps[S_TILE, hf][:], ACT.Square, scale=-1.0,
+                z_tiles[hf][:, SCALAR_TILE, :], h_ps[SCALAR_TILE, hf][:], ACT.Square, scale=-1.0,
                 bias=s_stats[:, hf, 1:2], accum_out=s_stats[:, hf, 2:3],
             )
 
-        squares(0)
-        for t in (0, 1, 2, 3):
-            if t == S_TILE:
-                squares(1)
+        centred_squares(0)
+        for t in range(PACK):
+            if t == SCALAR_TILE:
+                centred_squares(1)
                 stats = s_stats
             else:
                 stats = keep.tile([P, HALVES, 6], F32, name="stats%d" % t)
@@ -194,39 +197,34 @@ def tile_picked_inorm_none_p_kernel(
                     nc.vector.bn_stats(stats[:, hf, :], h_ps[t, hf][:])
             nc.vector.bn_aggr(mv[:, t, 1:3], stats[:].rearrange("p a b -> p (a b)"))
             nc.scalar.activation(rstd[:, t : t + 1], mv[:, t, 2:3], ACT.Abs_reciprocal_sqrt, bias=EPS)
-            ab = keep.tile([P, 2], F32, name="ab%d" % t)
+            coef[t] = keep.tile([P, 2], F32, name="ab%d" % t)
             nc.vector.tensor_scalar(
-                ab[:], mv[:, t, 0:2], rstd[:, t : t + 1], neg_gam[:, t : t + 1], ALU.mult, ALU.mult
+                coef[t][:], mv[:, t, 0:2], rstd[:, t : t + 1], neg_gam[:, t : t + 1], ALU.mult, ALU.mult
             )
-            coef[t] = ab
 
         norm_scalar(0, 0, 0, BANK)
         norm_scalar(0, 1, 0, BANK)
         norm_scalar(2, 0, 0, BANK)
         for hf in range(HALVES):
-            nc.vector.tensor_scalar(
-                planes[hf][:, S_TILE, :], h_sb[:, hf, :],
-                coef[S_TILE][:, 0:1], coef[S_TILE][:, 1:2], ALU.mult, ALU.add,
-            )
-        norm_vector(3, 0, 0, CHUNK)
-        norm_scalar(3, 0, CHUNK, BANK)
+            norm_vector(SCALAR_TILE, hf, 0, BANK, h_sb[:, hf, :])
+        norm_vector(3, 0, 0, BANK // 2, h_ps[3, 0][:, 0 : BANK // 2])
+        norm_scalar(3, 0, BANK // 2, BANK)
         norm_scalar(2, 1, 0, BANK)
         norm_scalar(3, 1, 0, BANK)
 
-        pieces = ((0, 256), (256, 512), (512, 768), (768, 896), (896, 1024))
         z_bf = {}
 
-        def weave(copy, c):
-            lo, hi = pieces[c]
+        def interleave(copy, c):
+            lo, hi = PIECES[c]
             hf, c0 = divmod(lo, BANK)
             z_bf[c] = keep.tile([P, hi - lo, PACK], BF16, name="z_bf%d" % c, align_bytes=64)
             copy(
                 z_bf[c][:].rearrange("p (g i) t -> p g t i", i=4),
-                planes[hf][:, :, c0 : c0 + hi - lo].rearrange("p t (g i) -> p g t i", i=4),
+                z_tiles[hf][:, :, c0 : c0 + hi - lo].rearrange("p t (g i) -> p g t i", i=4),
             )
 
-        def finish(c, evac):
-            lo, hi = pieces[c]
+        def finish(c, copy_out):
+            lo, hi = PIECES[c]
             z_codes = keep.tile([P, hi - lo], U32, name="z_codes%d" % c, align_bytes=64)
             z_sc = keep.tile([P, hi - lo], U8, name="z_sc%d" % c, align_bytes=64)
             nc.vector.quantize_mx(
@@ -245,16 +243,16 @@ def tile_picked_inorm_none_p_kernel(
                 stop=True,
             )
             res = keep.tile([P, hi - lo], F32, name="res%d" % c)
-            evac(res[:], acc[:, 0 : hi - lo])
+            copy_out(res[:], acc[:, 0 : hi - lo])
             nc.sync.dma_start(out[:, lo:hi], res[:])
 
-        weave(nc.vector.tensor_copy, 0)
-        weave(nc.vector.tensor_copy, 1)
-        weave(nc.scalar.copy, 2)
+        interleave(nc.vector.tensor_copy, 0)
+        interleave(nc.vector.tensor_copy, 1)
+        interleave(nc.scalar.copy, 2)
         finish(0, nc.scalar.copy)
         finish(1, nc.scalar.copy)
-        weave(nc.vector.tensor_copy, 3)
-        weave(nc.vector.tensor_copy, 4)
+        interleave(nc.vector.tensor_copy, 3)
+        interleave(nc.vector.tensor_copy, 4)
         finish(2, nc.scalar.copy)
         finish(3, nc.scalar.copy)
         finish(4, nc.vector.tensor_copy)

@@ -25,7 +25,7 @@ X_FIRST = 1536
 ROW0, ROW_STEP = 11, 7
 W1_VECTOR = 76
 SCALAR_TILE = 1
-PIECES = ((0, 256), (256, 512), (512, 768), (768, 896), (896, 1024))
+PIECES = ((0, 256), (768, 1024), (512, 768), (256, 384), (384, 512))
 
 
 def tile_picked_inorm_none_p_kernel(
@@ -202,15 +202,17 @@ def tile_picked_inorm_none_p_kernel(
                 coef[t][:], mv[:, t, 0:2], rstd[:, t : t + 1], neg_gam[:, t : t + 1], ALU.mult, ALU.mult
             )
 
+        half = BANK // 2
         norm_scalar(0, 0, 0, BANK)
-        norm_scalar(0, 1, 0, BANK)
         norm_scalar(2, 0, 0, BANK)
-        for hf in range(HALVES):
-            norm_vector(SCALAR_TILE, hf, 0, BANK, h_sb[:, hf, :])
-        norm_vector(3, 0, 0, BANK // 2, h_ps[3, 0][:, 0 : BANK // 2])
-        norm_scalar(3, 0, BANK // 2, BANK)
         norm_scalar(2, 1, 0, BANK)
+        norm_vector(SCALAR_TILE, 0, 0, BANK, h_sb[:, 0, :])
+        norm_vector(0, 1, 0, half, h_ps[0, 1][:, 0:half])
+        norm_vector(3, 0, 0, half, h_ps[3, 0][:, 0:half])
+        norm_vector(SCALAR_TILE, 1, 0, BANK, h_sb[:, 1, :])
+        norm_vector(0, 1, half, BANK, h_ps[0, 1][:, half:BANK])
         norm_scalar(3, 1, 0, BANK)
+        norm_scalar(3, 0, half, BANK)
 
         z_bf = {}
 
@@ -249,10 +251,10 @@ def tile_picked_inorm_none_p_kernel(
         interleave(nc.vector.tensor_copy, 0)
         interleave(nc.vector.tensor_copy, 1)
         interleave(nc.scalar.copy, 2)
+        interleave(nc.scalar.copy, 3)
         finish(0, nc.scalar.copy)
         finish(1, nc.scalar.copy)
-        interleave(nc.vector.tensor_copy, 3)
-        interleave(nc.vector.tensor_copy, 4)
         finish(2, nc.scalar.copy)
+        interleave(nc.vector.tensor_copy, 4)
         finish(3, nc.scalar.copy)
         finish(4, nc.vector.tensor_copy)

@@ -21,11 +21,9 @@ PACK = 4
 BANK = 512
 HALVES = S // BANK
 PASS = 128
-X_FIRST = 1536
+WARM_PASSES, WARM_M = 4, 64
 ROW0, ROW_STEP = 11, 7
-W1_VECTOR = 76
-SCALAR_TILE = 1
-PIECES = ((0, 256), (768, 1024), (512, 768), (256, 384), (384, 512))
+PIECES = ((0, 256), (256, 512), (512, 768), (768, 896), (896, 1024))
 
 
 def tile_picked_inorm_none_p_kernel(
@@ -43,38 +41,63 @@ def tile_picked_inorm_none_p_kernel(
 
         mv = keep.tile([P, PACK, 4], F32, name="mv")
         nc.vector.memset(mv[:, :, 0:1], -1.0)
-        nc.vector.memset(mv[:, SCALAR_TILE, 0:1], -float(BANK))
+        nc.vector.memset(mv[:, :, 1:2], -float(BANK))
         rstd = keep.tile([P, PACK], F32, name="rstd")
         nc.scalar.activation(rstd[:, 0:1], mv[:, 0, 0:1], ACT.Abs_reciprocal_sqrt, bias=EPS)
-        s_stats = keep.tile([P, HALVES, 3], F32, name="s_stats")
-        nc.vector.memset(s_stats[:, :, 0:1], float(BANK))
+        stats = keep.tile([P, PACK, 12], F32, name="stats")
+        nc.vector.memset(stats[:, 0:3, 3:4], float(BANK))
 
-        xw_all = keep.tile([P, T], U32, name="xw_all", align_bytes=64)
-        x_rows = x_words[0].rearrange("p c r -> p (c r)").bitcast(I32)
-        nc.sync.dma_start(xw_all[:, 0:X_FIRST].bitcast(I32), x_rows[:, 0:X_FIRST])
+        w1_raw = keep.tile([P, PACK, H], F32, name="w1_raw", align_bytes=64)
+        nc.sync.dma_start(w1_raw[:], w1.rearrange("(p j) c -> p j c", j=PACK))
         nc.sync.dma_start(offsets[:], offs)
         nc.sync.dma_start(
             xs_all[ROW0 : ROW0 + 15 * ROW_STEP + 1 : ROW_STEP, :].bitcast(I32),
             x_scales[0].bitcast(I32),
         )
-        nc.sync.dma_start(xw_all[:, X_FIRST:T].bitcast(I32), x_rows[:, X_FIRST:T])
-
-        w1_raw = keep.tile([P, PACK, H], F32, name="w1_raw", tag="w1_raw", align_bytes=64)
-        nc.sync.dma_start(w1_raw[:], w1.rearrange("(p j) c -> p j c", j=PACK))
+        xw_all = keep.tile([P, T], U32, name="xw_all", tag="xw_all", align_bytes=64)
+        nc.sync.dma_start(xw_all[:].bitcast(I32), x_words[0].rearrange("p c r -> p (c r)").bitcast(I32))
 
         gam = keep.tile([P, PACK], F32, name="gam")
         nc.sync.dma_start(gam[:], gamma.rearrange("(p t) o -> p (t o)", t=PACK))
 
-        xs = keep.tile([P, S], U8, name="xs", align_bytes=64)
-        nc.gpsimd.memset(xs[:].bitcast(I32), 0)
+        w1_bf = keep.tile([P, PACK, P, PACK], BF16, name="w1_bf", align_bytes=64)
+        w1_codes = keep.tile([P, H], U32, name="w1_codes", align_bytes=64)
+        w1_sc = keep.tile([P, H], U8, name="w1_sc", align_bytes=64)
+        nc.scalar.copy(
+            w1_bf[:].rearrange("p t m j -> p m j t"),
+            w1_raw[:].rearrange("p j (m t) -> p m j t", t=PACK),
+        )
 
-        xs_picked = keep.tile([P, S], U8, name="xs_picked", align_bytes=64)
+        xs = keep.tile([P, S], U8, name="xs", align_bytes=64)
+        nc.vector.memset(xs[:].bitcast(I32), 0)
+
+        xs_picked = keep.tile([P, S], U8, name="xs_picked", tag="xs_picked", align_bytes=64)
         nc.vector.tensor_copy(xs_picked[:], xs_all[:].indirect(offsets[:]))
         for q in range(4):
             first = ROW0 + 4 * q * ROW_STEP
-            nc.scalar.dma_start(
+            nc.sync.dma_start(
                 xs[32 * q : 32 * q + 4, :].bitcast(I32),
                 xs_picked[first : first + 3 * ROW_STEP + 1 : ROW_STEP, :].bitcast(I32),
+            )
+
+        nc.vector.quantize_mx(
+            out=w1_codes[:].bitcast(FP8X4),
+            scales=w1_sc[:],
+            in_=w1_bf[:].rearrange("p t m j -> p (t m j)"),
+        )
+        neg_gam = keep.tile([P, PACK], F32, name="neg_gam")
+        nc.scalar.activation(neg_gam[:], gam[:], ACT.Copy, scale=-1.0)
+
+        warm = psum.tile([P, BANK], F32, name="warm", tag="bank7")
+        for warm_pass in range(WARM_PASSES):
+            nc.tensor.matmul_mx(
+                out=warm[0:WARM_M, :],
+                lhsT=w1_codes[:, 0:WARM_M].bitcast(FP8X4),
+                lhsT_scale=w1_sc[:, 0:WARM_M],
+                rhs=w1_codes[:].bitcast(FP8X4),
+                rhs_scale=w1_sc[:],
+                start=True,
+                stop=True,
             )
 
         xw = []
@@ -84,63 +107,21 @@ def tile_picked_inorm_none_p_kernel(
             nc.vector.tensor_copy(picked[:], xw_all[:].indirect(offsets[:, entries]))
             xw.append(picked)
 
-        warm = psum.tile([P, BANK], F32, name="warm", tag="bank7")
-        for width in (BANK, BANK, BANK // 2):
-            nc.tensor.matmul_mx(
-                out=warm[:, 0:width],
-                lhsT=xw[0][:, 0:P].bitcast(FP8X4),
-                lhsT_scale=xs_picked[:, 0:P],
-                rhs=xw[0][:, 0:width].bitcast(FP8X4),
-                rhs_scale=xs_picked[:, 0:width],
-                start=True,
-                stop=True,
-            )
-
-        w1_bf = keep.tile([P, PACK, P, PACK], BF16, name="w1_bf", align_bytes=64)
-        w1_codes = keep.tile([P, H], U32, name="w1_codes", align_bytes=64)
-        w1_sc = keep.tile([P, H], U8, name="w1_sc", align_bytes=64)
-        w1_dealt = w1_raw[:].rearrange("p j (m t) -> p m j t", t=PACK)
-
-        def round_w1(copy, pair, lo, hi):
-            copy(
-                w1_bf[:, 2 * pair : 2 * pair + 2, lo:hi, :].rearrange("p t m j -> p m j t"),
-                w1_dealt[:, lo:hi, :, 2 * pair : 2 * pair + 2],
-            )
-
-        def quantise_w1(first_tile, end_tile):
-            cols = slice(first_tile * P, end_tile * P)
-            nc.vector.quantize_mx(
-                out=w1_codes[:, cols].bitcast(FP8X4),
-                scales=w1_sc[:, cols],
-                in_=w1_bf[:, first_tile:end_tile, :, :].rearrange("p t m j -> p (t m j)"),
-            )
-
-        round_w1(nc.vector.tensor_copy, 0, 0, W1_VECTOR)
-        round_w1(nc.scalar.copy, 0, W1_VECTOR, P)
-        round_w1(nc.scalar.copy, 1, W1_VECTOR, P)
-        round_w1(nc.vector.tensor_copy, 1, 0, W1_VECTOR // 2)
-        quantise_w1(1, 2)
-        quantise_w1(0, 1)
-        round_w1(nc.vector.tensor_copy, 1, W1_VECTOR // 2, W1_VECTOR)
-        quantise_w1(2, 4)
-        neg_gam = keep.tile([P, PACK], F32, name="neg_gam")
-        nc.scalar.activation(neg_gam[:], gam[:], ACT.Copy, scale=-1.0)
-
-        w2_sc = keep.tile([P, N], U8, name="w2_sc", tag="xs_all", align_bytes=64)
+        w2_sc = keep.tile([P, N], U8, name="w2_sc", tag="xs_picked", align_bytes=64)
         nc.gpsimd.memset(w2_sc[:].bitcast(I32), 0)
         for q in range(4):
             nc.sync.dma_start(
                 w2_sc[32 * q : 32 * q + 4, :].bitcast(I32),
                 w2_scales[0][4 * q : 4 * q + 4, :].bitcast(I32),
             )
-        w2_codes = keep.tile([P, N], U32, name="w2_codes", tag="w1_raw", align_bytes=64)
+        w2_codes = keep.tile([P, N], U32, name="w2_codes", tag="xw_all", align_bytes=64)
         nc.sync.dma_start(
             w2_codes[:].bitcast(I32),
             w2_words[0].rearrange("p c r -> p (c r)").bitcast(I32),
         )
 
         h_ps = {}
-        for t, hf in ((1, 0), (0, 0), (1, 1), (0, 1), (2, 0), (2, 1), (3, 0), (3, 1)):
+        for t, hf in ((1, 0), (3, 0), (0, 0), (2, 0), (1, 1), (0, 1), (2, 1), (3, 1)):
             cols = slice(t * P, (t + 1) * P)
             bank = psum.tile([P, BANK], F32, name="h%d_%d" % (t, hf), tag="bank%d" % (t * HALVES + hf))
             for lo in range(0, BANK, PASS):
@@ -160,59 +141,65 @@ def tile_picked_inorm_none_p_kernel(
             for hf in range(HALVES)
         ]
         coef = {}
+        h_sb = {}
 
         def norm_scalar(t, hf, lo, hi):
             nc.scalar.activation(
                 z_tiles[hf][:, t, lo:hi], h_ps[t, hf][:, lo:hi], ACT.Identity,
-                bias=coef[t][:, 1:2], scale=coef[t][:, 0:1],
+                bias=coef[t][:, 2:3], scale=coef[t][:, 0:1],
             )
 
-        def norm_vector(t, hf, lo, hi, source):
+        def norm_vector(t, hf, lo, hi):
             nc.vector.tensor_scalar(
-                z_tiles[hf][:, t, lo:hi], source,
-                coef[t][:, 0:1], coef[t][:, 1:2], ALU.mult, ALU.add,
+                z_tiles[hf][:, t, lo:hi], h_ps[t, hf][:, lo:hi],
+                coef[t][:, 0:1], coef[t][:, 2:3], ALU.mult, ALU.add,
             )
 
-        h_sb = keep.tile([P, HALVES, BANK], F32, name="h_sb", align_bytes=64)
-        for hf in range(HALVES):
-            nc.scalar.activation(
-                h_sb[:, hf, :], h_ps[SCALAR_TILE, hf][:], ACT.Copy, scale=1.0 / BANK,
-                accum_out=s_stats[:, hf, 1:2],
-            )
-
-        def centred_squares(hf):
-            nc.scalar.activation(
-                z_tiles[hf][:, SCALAR_TILE, :], h_ps[SCALAR_TILE, hf][:], ACT.Square, scale=-1.0,
-                bias=s_stats[:, hf, 1:2], accum_out=s_stats[:, hf, 2:3],
-            )
-
-        centred_squares(0)
-        for t in range(PACK):
-            if t == SCALAR_TILE:
-                centred_squares(1)
-                stats = s_stats
-            else:
-                stats = keep.tile([P, HALVES, 6], F32, name="stats%d" % t)
-                for hf in range(HALVES):
-                    nc.vector.bn_stats(stats[:, hf, :], h_ps[t, hf][:])
-            nc.vector.bn_aggr(mv[:, t, 1:3], stats[:].rearrange("p a b -> p (a b)"))
-            nc.scalar.activation(rstd[:, t : t + 1], mv[:, t, 2:3], ACT.Abs_reciprocal_sqrt, bias=EPS)
-            coef[t] = keep.tile([P, 2], F32, name="ab%d" % t)
+        def norm_copy(t):
             nc.vector.tensor_scalar(
-                coef[t][:], mv[:, t, 0:2], rstd[:, t : t + 1], neg_gam[:, t : t + 1], ALU.mult, ALU.mult
+                z_tiles[0][:, t, :], h_sb[t][:], coef[t][:, 1:2], coef[t][:, 2:3], ALU.mult, ALU.add,
             )
 
-        half = BANK // 2
-        norm_scalar(0, 0, 0, BANK)
-        norm_scalar(2, 0, 0, BANK)
-        norm_scalar(2, 1, 0, BANK)
-        norm_vector(SCALAR_TILE, 0, 0, BANK, h_sb[:, 0, :])
-        norm_vector(0, 1, 0, half, h_ps[0, 1][:, 0:half])
-        norm_vector(3, 0, 0, half, h_ps[3, 0][:, 0:half])
-        norm_vector(SCALAR_TILE, 1, 0, BANK, h_sb[:, 1, :])
-        norm_vector(0, 1, half, BANK, h_ps[0, 1][:, half:BANK])
+        def copy_and_mean(t):
+            h_sb[t] = keep.tile([P, BANK], F32, name="h_sb%d" % t, align_bytes=64)
+            nc.scalar.activation(
+                h_sb[t][:], h_ps[t, 0][:], ACT.Copy, scale=1.0 / BANK, accum_out=stats[:, t, 4:5]
+            )
+
+        def centred_squares(t):
+            nc.scalar.activation(
+                z_tiles[0][:, t, :], h_ps[t, 0][:], ACT.Square, scale=-1.0,
+                bias=stats[:, t, 4:5], accum_out=stats[:, t, 5:6],
+            )
+
+        def vector_stats(t, hf):
+            nc.vector.bn_stats(stats[:, t, 6 * hf : 6 * hf + 6], h_ps[t, hf][:])
+
+        def coefficients(t, first):
+            nc.vector.bn_aggr(mv[:, t, 2:4], stats[:, t, first:12])
+            nc.scalar.activation(rstd[:, t : t + 1], mv[:, t, 3:4], ACT.Abs_reciprocal_sqrt, bias=EPS)
+            coef[t] = keep.tile([P, 3], F32, name="coef%d" % t)
+            nc.vector.tensor_scalar(
+                coef[t][:], mv[:, t, 0:3], rstd[:, t : t + 1], neg_gam[:, t : t + 1], ALU.mult, ALU.mult
+            )
+
+        vector_stats(3, 0)
+        for t in (1, 0, 2):
+            copy_and_mean(t)
+            centred_squares(t)
+            vector_stats(t, 1)
+            coefficients(t, 3)
+        vector_stats(3, 1)
+        coefficients(3, 0)
+
+        norm_copy(1)
+        norm_copy(0)
+        norm_copy(2)
+        norm_vector(3, 0, 0, BANK)
+        norm_scalar(1, 1, 0, BANK)
+        norm_scalar(0, 1, 0, BANK)
         norm_scalar(3, 1, 0, BANK)
-        norm_scalar(3, 0, half, BANK)
+        norm_scalar(2, 1, 0, BANK)
 
         z_bf = {}
 
@@ -234,16 +221,17 @@ def tile_picked_inorm_none_p_kernel(
                 scales=z_sc[:],
                 in_=z_bf[c][:].rearrange("p n t -> p (n t)"),
             )
-            acc = psum.tile([P, BANK], F32, name="acc%d" % c, tag="bank%d" % c)
-            nc.tensor.matmul_mx(
-                out=acc[:, 0 : hi - lo],
-                lhsT=w2_codes[:].bitcast(FP8X4),
-                lhsT_scale=w2_sc[:],
-                rhs=z_codes[:].bitcast(FP8X4),
-                rhs_scale=z_sc[:],
-                start=True,
-                stop=True,
-            )
+            acc = psum.tile([P, BANK], F32, name="acc%d" % c, tag="bank%d" % (2, 0, 4, 6, 3)[c])
+            for c0 in range(0, hi - lo, PASS):
+                nc.tensor.matmul_mx(
+                    out=acc[:, c0 : c0 + PASS],
+                    lhsT=w2_codes[:].bitcast(FP8X4),
+                    lhsT_scale=w2_sc[:],
+                    rhs=z_codes[:, c0 : c0 + PASS].bitcast(FP8X4),
+                    rhs_scale=z_sc[:, c0 : c0 + PASS],
+                    start=True,
+                    stop=True,
+                )
             res = keep.tile([P, hi - lo], F32, name="res%d" % c)
             copy_out(res[:], acc[:, 0 : hi - lo])
             nc.sync.dma_start(out[:, lo:hi], res[:])

@@ -75,7 +75,7 @@ def tile_picked_inorm_none_p_kernel(
         nc.vector.tensor_copy(xs_picked[:], xs_all[:].indirect(offsets[:]))
         for q in range(4):
             first = ROW0 + 4 * q * ROW_STEP
-            nc.sync.dma_start(
+            nc.scalar.dma_start(
                 xs[32 * q : 32 * q + 4, :].bitcast(I32),
                 xs_picked[first : first + 3 * ROW_STEP + 1 : ROW_STEP, :].bitcast(I32),
             )

@@ -21,7 +21,7 @@ PACK = 4
 BANK = 512
 HALVES = S // BANK
 PASS = 128
-WARM_PASSES, WARM_M = 4, 64
+WARM_PASSES, WARM_M = 3, 64
 ROW0, ROW_STEP = 11, 7
 PIECES = ((0, 256), (256, 512), (512, 768), (768, 896), (896, 1024))
 
@@ -63,10 +63,10 @@ def tile_picked_inorm_none_p_kernel(
         w1_bf = keep.tile([P, PACK, P, PACK], BF16, name="w1_bf", align_bytes=64)
         w1_codes = keep.tile([P, H], U32, name="w1_codes", align_bytes=64)
         w1_sc = keep.tile([P, H], U8, name="w1_sc", align_bytes=64)
-        nc.scalar.copy(
-            w1_bf[:].rearrange("p t m j -> p m j t"),
-            w1_raw[:].rearrange("p j (m t) -> p m j t", t=PACK),
-        )
+        w1_dealt = w1_raw[:].rearrange("p j (m t) -> p m j t", t=PACK)
+        for pair in range(2):
+            tiles = slice(2 * pair, 2 * pair + 2)
+            nc.scalar.copy(w1_bf[:, tiles, :, :].rearrange("p t m j -> p m j t"), w1_dealt[:, :, :, tiles])
 
         xs = keep.tile([P, S], U8, name="xs", align_bytes=64)
         nc.vector.memset(xs[:].bitcast(I32), 0)

@@ -21,7 +21,7 @@ PACK = 4
 BANK = 512
 HALVES = S // BANK
 PASS = 128
-WARM_PASSES, WARM_M = 3, 64
+WARM_PASSES, WARM_M = 3, 32
 ROW0, ROW_STEP = 11, 7
 PIECES = ((0, 256), (256, 512), (512, 768), (768, 896), (896, 1024))
 
@@ -121,7 +121,7 @@ def tile_picked_inorm_none_p_kernel(
         )
 
         h_ps = {}
-        for t, hf in ((1, 0), (3, 0), (0, 0), (2, 0), (1, 1), (0, 1), (2, 1), (3, 1)):
+        for t, hf in ((1, 0), (3, 0), (0, 0), (2, 0), (1, 1), (0, 1), (3, 1), (2, 1)):
             cols = slice(t * P, (t + 1) * P)
             bank = psum.tile([P, BANK], F32, name="h%d_%d" % (t, hf), tag="bank%d" % (t * HALVES + hf))
             for lo in range(0, BANK, PASS):
@@ -137,7 +137,7 @@ def tile_picked_inorm_none_p_kernel(
             h_ps[t, hf] = bank
 
         z_tiles = [
-            keep.tile([P, PACK, BANK], BF16, name="planes%d" % hf, align_bytes=64)
+            keep.tile([P, PACK, BANK], BF16, name="planes%d" % hf, tag="planes%d" % hf, align_bytes=64)
             for hf in range(HALVES)
         ]
         coef = {}
@@ -155,8 +155,8 @@ def tile_picked_inorm_none_p_kernel(
                 coef[t][:, 0:1], coef[t][:, 2:3], ALU.mult, ALU.add,
             )
 
-        def norm_copy(t):
-            nc.vector.tensor_scalar(
+        def norm_copy(engine, t):
+            engine.tensor_scalar(
                 z_tiles[0][:, t, :], h_sb[t][:], coef[t][:, 1:2], coef[t][:, 2:3], ALU.mult, ALU.add,
             )
 
@@ -178,35 +178,37 @@ def tile_picked_inorm_none_p_kernel(
         def coefficients(t, first):
             nc.vector.bn_aggr(mv[:, t, 2:4], stats[:, t, first:12])
             nc.scalar.activation(rstd[:, t : t + 1], mv[:, t, 3:4], ACT.Abs_reciprocal_sqrt, bias=EPS)
-            coef[t] = keep.tile([P, 3], F32, name="coef%d" % t)
+            twice = keep.tile([P, 3, 2], F32, name="coef%d" % t)
+            coef[t] = twice[:, :, 0]
             nc.vector.tensor_scalar(
-                coef[t][:], mv[:, t, 0:3], rstd[:, t : t + 1], neg_gam[:, t : t + 1], ALU.mult, ALU.mult
+                twice[:], mv[:, t, 0:3].unsqueeze(2).to_broadcast([P, 3, 2]), rstd[:, t : t + 1], neg_gam[:, t : t + 1], ALU.mult, ALU.mult
             )
 
         vector_stats(3, 0)
-        for t in (1, 0, 2):
+        for t in (1, 0):
             copy_and_mean(t)
             centred_squares(t)
             vector_stats(t, 1)
             coefficients(t, 3)
+        copy_and_mean(2)
+        centred_squares(2)
         vector_stats(3, 1)
         coefficients(3, 0)
-
-        norm_copy(1)
-        norm_copy(0)
-        norm_copy(2)
+        vector_stats(2, 1)
+        norm_copy(nc.gpsimd, 1)
+        norm_copy(nc.gpsimd, 0)
         norm_vector(3, 0, 0, BANK)
-        norm_scalar(1, 1, 0, BANK)
-        norm_scalar(0, 1, 0, BANK)
-        norm_scalar(3, 1, 0, BANK)
-        norm_scalar(2, 1, 0, BANK)
+        coefficients(2, 3)
+        norm_copy(nc.vector, 2)
+        for t in (1, 0, 3, 2):
+            norm_scalar(t, 1, 0, BANK)
 
         z_bf = {}
 
         def interleave(copy, c):
             lo, hi = PIECES[c]
             hf, c0 = divmod(lo, BANK)
-            z_bf[c] = keep.tile([P, hi - lo, PACK], BF16, name="z_bf%d" % c, align_bytes=64)
+            z_bf[c] = keep.tile([P, hi - lo, PACK], BF16, name="z_bf%d" % c, tag="z_bf%d" % (c % 4), align_bytes=64)
             copy(
                 z_bf[c][:].rearrange("p (g i) t -> p g t i", i=4),
                 z_tiles[hf][:, :, c0 : c0 + hi - lo].rearrange("p t (g i) -> p g t i", i=4),
@@ -214,7 +216,8 @@ def tile_picked_inorm_none_p_kernel(
 
         def finish(c, copy_out):
             lo, hi = PIECES[c]
-            z_codes = keep.tile([P, hi - lo], U32, name="z_codes%d" % c, align_bytes=64)
+            tag = {2: "planes0", 3: "z_bf1"}.get(c, "z_codes%d" % c)
+            z_codes = keep.tile([P, hi - lo], U32, name="z_codes%d" % c, tag=tag, align_bytes=64)
             z_sc = keep.tile([P, hi - lo], U8, name="z_sc%d" % c, align_bytes=64)
             nc.vector.quantize_mx(
                 out=z_codes[:].bitcast(FP8X4),

@@ -22,7 +22,8 @@ BANK = 512
 HALVES = S // BANK
 PASS = 128
 WARM_PASSES, WARM_M = 3, 32
-ROW0, ROW_STEP = 11, 7
+ROW0, ROW_STEP = 4, 8
+PITCH = BANK + 8
 PIECES = ((0, 256), (256, 512), (512, 768), (768, 896), (896, 1024))
 
 
@@ -137,7 +138,7 @@ def tile_picked_inorm_none_p_kernel(
             h_ps[t, hf] = bank
 
         z_tiles = [
-            keep.tile([P, PACK, BANK], BF16, name="planes%d" % hf, tag="planes%d" % hf, align_bytes=64)
+            keep.tile([P, PACK, PITCH], BF16, name="planes%d" % hf, tag="planes%d" % hf, align_bytes=64)
             for hf in range(HALVES)
         ]
         coef = {}
@@ -157,7 +158,7 @@ def tile_picked_inorm_none_p_kernel(
 
         def norm_copy(engine, t):
             engine.tensor_scalar(
-                z_tiles[0][:, t, :], h_sb[t][:], coef[t][:, 1:2], coef[t][:, 2:3], ALU.mult, ALU.add,
+                z_tiles[0][:, t, 0:BANK], h_sb[t][:], coef[t][:, 1:2], coef[t][:, 2:3], ALU.mult, ALU.add,
             )
 
         def copy_and_mean(t):
@@ -168,7 +169,7 @@ def tile_picked_inorm_none_p_kernel(
 
         def centred_squares(t):
             nc.scalar.activation(
-                z_tiles[0][:, t, :], h_ps[t, 0][:], ACT.Square, scale=-1.0,
+                z_tiles[0][:, t, 0:BANK], h_ps[t, 0][:], ACT.Square, scale=-1.0,
                 bias=stats[:, t, 4:5], accum_out=stats[:, t, 5:6],
             )
 

from contextlib import ExitStack

import concourse.mybir as mybir

K, T, S, H, N = 512, 4096, 1024, 512, 128
FLOPS = 2 * K * H * S + 2 * H * N * S
EPS = 1e-5

F32 = mybir.dt.float32
BF16 = mybir.dt.bfloat16
I32 = mybir.dt.int32
U32 = mybir.dt.uint32
U16 = mybir.dt.uint16
U8 = mybir.dt.uint8
FP8X4 = mybir.dt.float8_e4m3fn_x4
ACT = mybir.ActivationFunctionType
ALU = mybir.AluOpType

P = 128
PACK = 4
BANK = 512
HALVES = S // BANK
PASS = 128
WARM_PASSES, WARM_M = 3, 32
ROW0, ROW_STEP = 4, 8
PITCH = BANK + 8
PIECES = ((0, 256), (256, 512), (512, 768), (768, 896), (896, 1024))


def tile_picked_inorm_none_p_kernel(
    tc, x_words, x_scales, w1, w2_words, w2_scales, gamma, offs, out
):
    nc = tc.nc
    with ExitStack() as ctx:
        keep = ctx.enter_context(tc.tile_pool(name="keep", bufs=1))
        psum = ctx.enter_context(tc.psum_pool(name="psum", bufs=1))

        offsets = keep.tile([P, S // 16], U16, name="offsets")

        xs_all = keep.tile([P, T], U8, name="xs_all", tag="xs_all", align_bytes=64)
        nc.vector.memset(xs_all[:].bitcast(I32), 0)

        mv = keep.tile([P, PACK, 4], F32, name="mv")
        nc.vector.memset(mv[:, :, 0:1], -1.0)
        nc.vector.memset(mv[:, :, 1:2], -float(BANK))
        rstd = keep.tile([P, PACK], F32, name="rstd")
        nc.scalar.activation(rstd[:, 0:1], mv[:, 0, 0:1], ACT.Abs_reciprocal_sqrt, bias=EPS)
        stats = keep.tile([P, PACK, 12], F32, name="stats")
        nc.vector.memset(stats[:, 0:3, 3:4], float(BANK))

        w1_raw = keep.tile([P, PACK, H], F32, name="w1_raw", align_bytes=64)
        nc.sync.dma_start(w1_raw[:], w1.rearrange("(p j) c -> p j c", j=PACK))
        nc.sync.dma_start(offsets[:], offs)
        nc.sync.dma_start(
            xs_all[ROW0 : ROW0 + 15 * ROW_STEP + 1 : ROW_STEP, :].bitcast(I32),
            x_scales[0].bitcast(I32),
        )
        xw_all = keep.tile([P, T], U32, name="xw_all", tag="xw_all", align_bytes=64)
        nc.sync.dma_start(xw_all[:].bitcast(I32), x_words[0].rearrange("p c r -> p (c r)").bitcast(I32))

        gam = keep.tile([P, PACK], F32, name="gam")
        nc.sync.dma_start(gam[:], gamma.rearrange("(p t) o -> p (t o)", t=PACK))

        w1_bf = keep.tile([P, PACK, P, PACK], BF16, name="w1_bf", align_bytes=64)
        w1_codes = keep.tile([P, H], U32, name="w1_codes", align_bytes=64)
        w1_sc = keep.tile([P, H], U8, name="w1_sc", align_bytes=64)
        w1_dealt = w1_raw[:].rearrange("p j (m t) -> p m j t", t=PACK)
        for pair in range(2):
            tiles = slice(2 * pair, 2 * pair + 2)
            nc.scalar.copy(w1_bf[:, tiles, :, :].rearrange("p t m j -> p m j t"), w1_dealt[:, :, :, tiles])

        xs = keep.tile([P, S], U8, name="xs", align_bytes=64)
        nc.vector.memset(xs[:].bitcast(I32), 0)

        xs_picked = keep.tile([P, S], U8, name="xs_picked", tag="xs_picked", align_bytes=64)
        nc.vector.tensor_copy(xs_picked[:], xs_all[:].indirect(offsets[:]))
        for q in range(4):
            first = ROW0 + 4 * q * ROW_STEP
            nc.scalar.dma_start(
                xs[32 * q : 32 * q + 4, :].bitcast(I32),
                xs_picked[first : first + 3 * ROW_STEP + 1 : ROW_STEP, :].bitcast(I32),
            )

        nc.vector.quantize_mx(
            out=w1_codes[:].bitcast(FP8X4),
            scales=w1_sc[:],
            in_=w1_bf[:].rearrange("p t m j -> p (t m j)"),
        )
        neg_gam = keep.tile([P, PACK], F32, name="neg_gam")
        nc.scalar.activation(neg_gam[:], gam[:], ACT.Copy, scale=-1.0)

        warm = psum.tile([P, BANK], F32, name="warm", tag="bank7")
        for warm_pass in range(WARM_PASSES):
            nc.tensor.matmul_mx(
                out=warm[0:WARM_M, :],
                lhsT=w1_codes[:, 0:WARM_M].bitcast(FP8X4),
                lhsT_scale=w1_sc[:, 0:WARM_M],
                rhs=w1_codes[:].bitcast(FP8X4),
                rhs_scale=w1_sc[:],
                start=True,
                stop=True,
            )

        xw = []
        for hf in range(HALVES):
            picked = keep.tile([P, BANK], U32, name="xw%d" % hf, align_bytes=64)
            entries = slice(hf * BANK // 16, (hf + 1) * BANK // 16)
            nc.vector.tensor_copy(picked[:], xw_all[:].indirect(offsets[:, entries]))
            xw.append(picked)

        w2_sc = keep.tile([P, N], U8, name="w2_sc", tag="xs_picked", align_bytes=64)
        nc.gpsimd.memset(w2_sc[:].bitcast(I32), 0)
        for q in range(4):
            nc.sync.dma_start(
                w2_sc[32 * q : 32 * q + 4, :].bitcast(I32),
                w2_scales[0][4 * q : 4 * q + 4, :].bitcast(I32),
            )
        w2_codes = keep.tile([P, N], U32, name="w2_codes", tag="xw_all", align_bytes=64)
        nc.sync.dma_start(
            w2_codes[:].bitcast(I32),
            w2_words[0].rearrange("p c r -> p (c r)").bitcast(I32),
        )

        h_ps = {}
        for t, hf in ((1, 0), (3, 0), (0, 0), (2, 0), (1, 1), (0, 1), (3, 1), (2, 1)):
            cols = slice(t * P, (t + 1) * P)
            bank = psum.tile([P, BANK], F32, name="h%d_%d" % (t, hf), tag="bank%d" % (t * HALVES + hf))
            for lo in range(0, BANK, PASS):
                nc.tensor.matmul_mx(
                    out=bank[:, lo : lo + PASS],
                    lhsT=w1_codes[:, cols].bitcast(FP8X4),
                    lhsT_scale=w1_sc[:, cols],
                    rhs=xw[hf][:, lo : lo + PASS].bitcast(FP8X4),
                    rhs_scale=xs[:, hf * BANK + lo : hf * BANK + lo + PASS],
                    start=True,
                    stop=True,
                )
            h_ps[t, hf] = bank

        z_tiles = [
            keep.tile([P, PACK, PITCH], BF16, name="planes%d" % hf, tag="planes%d" % hf, align_bytes=64)
            for hf in range(HALVES)
        ]
        coef = {}
        h_sb = {}

        def norm_scalar(t, hf, lo, hi):
            nc.scalar.activation(
                z_tiles[hf][:, t, lo:hi], h_ps[t, hf][:, lo:hi], ACT.Identity,
                bias=coef[t][:, 2:3], scale=coef[t][:, 0:1],
            )

        def norm_vector(t, hf, lo, hi):
            nc.vector.tensor_scalar(
                z_tiles[hf][:, t, lo:hi], h_ps[t, hf][:, lo:hi],
                coef[t][:, 0:1], coef[t][:, 2:3], ALU.mult, ALU.add,
            )

        def norm_copy(engine, t):
            engine.tensor_scalar(
                z_tiles[0][:, t, 0:BANK], h_sb[t][:], coef[t][:, 1:2], coef[t][:, 2:3], ALU.mult, ALU.add,
            )

        def copy_and_mean(t):
            h_sb[t] = keep.tile([P, BANK], F32, name="h_sb%d" % t, align_bytes=64)
            nc.scalar.activation(
                h_sb[t][:], h_ps[t, 0][:], ACT.Copy, scale=1.0 / BANK, accum_out=stats[:, t, 4:5]
            )

        def centred_squares(t):
            nc.scalar.activation(
                z_tiles[0][:, t, 0:BANK], h_ps[t, 0][:], ACT.Square, scale=-1.0,
                bias=stats[:, t, 4:5], accum_out=stats[:, t, 5:6],
            )

        def vector_stats(t, hf):
            nc.vector.bn_stats(stats[:, t, 6 * hf : 6 * hf + 6], h_ps[t, hf][:])

        def coefficients(t, first):
            nc.vector.bn_aggr(mv[:, t, 2:4], stats[:, t, first:12])
            nc.scalar.activation(rstd[:, t : t + 1], mv[:, t, 3:4], ACT.Abs_reciprocal_sqrt, bias=EPS)
            twice = keep.tile([P, 3, 2], F32, name="coef%d" % t)
            coef[t] = twice[:, :, 0]
            nc.vector.tensor_scalar(
                twice[:], mv[:, t, 0:3].unsqueeze(2).to_broadcast([P, 3, 2]), rstd[:, t : t + 1], neg_gam[:, t : t + 1], ALU.mult, ALU.mult
            )

        vector_stats(3, 0)
        for t in (1, 0):
            copy_and_mean(t)
            centred_squares(t)
            vector_stats(t, 1)
            coefficients(t, 3)
        copy_and_mean(2)
        centred_squares(2)
        vector_stats(3, 1)
        coefficients(3, 0)
        vector_stats(2, 1)
        norm_copy(nc.gpsimd, 1)
        norm_copy(nc.gpsimd, 0)
        norm_vector(3, 0, 0, BANK)
        coefficients(2, 3)
        norm_copy(nc.vector, 2)
        for t in (1, 0, 3, 2):
            norm_scalar(t, 1, 0, BANK)

        z_bf = {}

        def interleave(copy, c):
            lo, hi = PIECES[c]
            hf, c0 = divmod(lo, BANK)
            z_bf[c] = keep.tile([P, hi - lo, PACK], BF16, name="z_bf%d" % c, tag="z_bf%d" % (c % 4), align_bytes=64)
            copy(
                z_bf[c][:].rearrange("p (g i) t -> p g t i", i=4),
                z_tiles[hf][:, :, c0 : c0 + hi - lo].rearrange("p t (g i) -> p g t i", i=4),
            )

        def finish(c, copy_out):
            lo, hi = PIECES[c]
            tag = {2: "planes0", 3: "z_bf1"}.get(c, "z_codes%d" % c)
            z_codes = keep.tile([P, hi - lo], U32, name="z_codes%d" % c, tag=tag, align_bytes=64)
            z_sc = keep.tile([P, hi - lo], U8, name="z_sc%d" % c, align_bytes=64)
            nc.vector.quantize_mx(
                out=z_codes[:].bitcast(FP8X4),
                scales=z_sc[:],
                in_=z_bf[c][:].rearrange("p n t -> p (n t)"),
            )
            acc = psum.tile([P, BANK], F32, name="acc%d" % c, tag="bank%d" % (2, 0, 4, 6, 3)[c])
            for c0 in range(0, hi - lo, PASS):
                nc.tensor.matmul_mx(
                    out=acc[:, c0 : c0 + PASS],
                    lhsT=w2_codes[:].bitcast(FP8X4),
                    lhsT_scale=w2_sc[:],
                    rhs=z_codes[:, c0 : c0 + PASS].bitcast(FP8X4),
                    rhs_scale=z_sc[:, c0 : c0 + PASS],
                    start=True,
                    stop=True,
                )
            res = keep.tile([P, hi - lo], F32, name="res%d" % c)
            copy_out(res[:], acc[:, 0 : hi - lo])
            nc.sync.dma_start(out[:, lo:hi], res[:])

        interleave(nc.vector.tensor_copy, 0)
        interleave(nc.vector.tensor_copy, 1)
        interleave(nc.scalar.copy, 2)
        interleave(nc.scalar.copy, 3)
        finish(0, nc.scalar.copy)
        finish(1, nc.scalar.copy)
        finish(2, nc.scalar.copy)
        interleave(nc.vector.tensor_copy, 4)
        finish(3, nc.scalar.copy)
        finish(4, nc.vector.tensor_copy)
